import numpy as np
import ml_dtypes


def mxq(x, axis, fmt="e4m3"):
    dtype, down = {"e4m3": (ml_dtypes.float8_e4m3fn, 7), "e5m2": (ml_dtypes.float8_e5m2, 14)}[fmt]
    v = np.moveaxis(np.asarray(x, np.float32).astype(ml_dtypes.bfloat16).astype(np.float64), axis, -1)
    blocks = v.reshape(v.shape[:-1] + (-1, 32))
    amax = np.abs(blocks).max(-1, keepdims=True)
    byte = np.maximum(np.where(amax > 0, np.frexp(amax)[1] - 1 + 127, 0) - down, 1)
    scale = np.exp2(byte - 127.0)
    codes = (blocks / scale).astype(np.float32).astype(dtype).astype(np.float64)
    return np.moveaxis((codes * scale).reshape(v.shape), -1, axis)


WIDE = False


def mx_kscale(k):
    if not WIDE:
        return np.ones(k)
    levels = np.array([10, -10, 5, -5, 0])
    if k % 512:
        return np.exp2(np.random.permutation(np.resize(levels, k // 32))).repeat(32)
    a = np.empty((k // 512, 16))
    for p in range(k // 512):
        a[p, :8] = np.random.permutation(np.resize(levels, 8))
        for g in range(8):
            far = levels[np.abs(levels - a[p, g]) >= 10]
            a[p, g + 8] = far[np.random.randint(len(far))]
    return np.exp2(a.ravel()).repeat(32)


def f64(x):
    return np.asarray(x).astype(np.float64)


def striped(idx):
    return np.tile(np.asarray(idx).reshape(-1, 16).T, (8, 1)).astype(np.uint16)


def unstriped(offs):
    return offs[:16].T.reshape(-1).astype(np.int64)


E2M1 = np.array([0.0, 0.5, 1.0, 1.5, 2.0, 3.0, 4.0, 6.0, -0.0, -0.5, -1.0, -1.5, -2.0, -3.0, -4.0, -6.0])


def pack_weight(w, fmt):
    k, n = w.shape
    w = f64(np.asarray(w, np.float32).astype(ml_dtypes.bfloat16)).reshape(k // 32, 32, n)
    amax = np.abs(w).max(1)
    if fmt == "e4m3":
        byte = np.frexp(amax)[1] - 1 + 127 - 7
    else:
        mant, ex = np.frexp(amax / 6.0)
        byte = np.where(mant > 0.5, ex, ex - 1) + 127
    byte = np.clip(np.where(amax > 0, byte, 1), 1, 254)
    scaled = (w * np.exp2(127.0 - byte)[:, None, :]).reshape(k, n).astype(np.float32)
    by_word = np.ascontiguousarray(scaled.reshape(k // 512, 128, 4, n).transpose(0, 1, 3, 2))
    if fmt == "e4m3":
        words = by_word.astype(ml_dtypes.float8_e4m3fn).view(np.uint8)
    else:
        c = by_word.astype(ml_dtypes.float4_e2m1fn).view(np.uint8) & 0xF
        words = (c[..., 0::2] | (c[..., 1::2] << 4)).reshape(k // 512, 128, 2 * n)
    return np.ascontiguousarray(words), np.ascontiguousarray(byte.astype(np.uint8).reshape(k // 512, 16, n))


def unpack_weight(words, scales, fmt):
    g, _, n = scales.shape
    words = np.ascontiguousarray(words).reshape(g, 128, n, -1)
    if fmt == "e4m3":
        vals = words.view(ml_dtypes.float8_e4m3fn).astype(np.float64)
    else:
        nib = np.empty((g, 128, n, 4), np.uint8)
        nib[..., 0::2] = words & 0xF
        nib[..., 1::2] = words >> 4
        vals = E2M1[nib]
    vals = vals * np.repeat(np.exp2(scales.astype(np.float64) - 127.0), 8, axis=1)[..., None]
    return vals.transpose(0, 1, 3, 2).reshape(g * 512, n)


K, T, S, J, I = 1024, 1024, 1024, 512, 512


def setup_inputs():
    n = np.random.standard_normal
    idx = np.random.permutation(T)[:J]
    idx2 = np.random.permutation(S)[:I]
    fk = mx_kscale(K)
    xap = pack_weight(n((K, T)) * 0.1 * fk[:, None], "e4m3")
    return {
        "xa_words": xap[0],
        "xa_scales": xap[1],
        "xb": (n((K, S)) / fk[:, None]).astype(np.float32),
        "cw1": (np.random.uniform(16.0, 64.0, (1, I))).astype(np.float32),
        "offs": striped(idx),
        "offs2": striped(idx2),
    }


def reference(xa_words, xa_scales, xb, cw1, offs, offs2):
    idx = unstriped(offs)
    idx2 = unstriped(offs2)
    xau = unpack_weight(xa_words, xa_scales, "e4m3")
    xaidxg = xau[:, idx]
    xbidx2q = mxq(f64(xb)[:, idx2], 0, "e4m3")
    a = xaidxg.T @ xbidx2q
    r = np.maximum(a, 0.0)
    y = r * f64(cw1) / (np.sum(r, axis=1, keepdims=True) + 1.0)
    return y

@@ -1,0 +1,178 @@
+from contextlib import ExitStack
+
+import concourse.mybir as mybir
+from concourse.masks import make_identity
+
+K, T, S, J, I = 1024, 1024, 1024, 512, 512
+FLOPS = 2 * K * J * I
+
+F32 = mybir.dt.float32
+BF16 = mybir.dt.bfloat16
+I32 = mybir.dt.int32
+U32 = mybir.dt.uint32
+U16 = mybir.dt.uint16
+U8 = mybir.dt.uint8
+FP8X4 = mybir.dt.float8_e4m3fn_x4
+ALU = mybir.AluOpType
+ACT = mybir.ActivationFunctionType
+
+P = 128
+PACK = 4
+PASSES = 2
+HALF = I // 2
+J_TILES = J // P
+LIST_ROWS = 16
+
+
+def tile_list_affinity_of_two_lists_kernel(tc, xa_words, xa_scales, xb, cw1, offs, offs2, out):
+    nc = tc.nc
+    with ExitStack() as ctx:
+        sb = ctx.enter_context(tc.tile_pool(name="sb", bufs=1))
+        ps = ctx.enter_context(tc.psum_pool(name="ps", bufs=1))
+
+        list_a = sb.tile([P, J // LIST_ROWS], U16, name="list_a")
+        list_b = sb.tile([P, I // LIST_ROWS], U16, name="list_b")
+        nc.sync.dma_start(list_a[:], offs)
+        nc.sync.dma_start(list_b[:], offs2)
+
+        a_words = [sb.tile([P, T], I32, name="a_words%d" % z) for z in range(PASSES)]
+
+        def load_a_words(z):
+            nc.sync.dma_start(a_words[z][:], xa_words[z].rearrange("p t r -> p (t r)").bitcast(I32))
+
+        a_scales = sb.tile([P, T], U8, name="a_scales")
+        nc.vector.memset(a_scales[:].bitcast(I32), 0)
+        for q in range(4):
+            nc.scalar.dma_start(
+                a_scales[32 * q : 32 * q + 4 * PASSES, :].bitcast(I32),
+                xa_scales[:, 4 * q : 4 * q + 4, :].bitcast(I32),
+            )
+        cw_rows = sb.tile([P, PACK], F32, name="cw_rows")
+        nc.scalar.dma_start(cw_rows[:], cw1.rearrange("o (p b) -> (o p) b", b=PACK))
+        identity = sb.tile([P, P], F32, name="identity")
+        make_identity(nc, identity[:])
+
+        xb_rows = xb.rearrange("(z p u e) s -> z u p e s", z=PASSES, u=2, e=2)
+        chunks = {(0, 0): [512, 512], (0, 1): [512, 512], (1, 0): [512, 512], (1, 1): [512, 384, 128]}
+        raw = {}
+
+        def load_b(z, u):
+            c0 = 0
+            for n, w in enumerate(chunks[(z, u)]):
+                t = sb.tile([P, 2, w], F32, name="b_raw%d%d%d" % (z, u, n))
+                nc.sync.dma_start(t[:], xb_rows[z, u, :, :, c0 : c0 + w])
+                raw[(z, u, n)] = (t, c0, w)
+                c0 += w
+
+        load_a_words(0)
+        for z in range(PASSES):
+            for u in range(2):
+                load_b(z, u)
+        load_a_words(1)
+
+        pairs = {}
+
+        def cast_b(z, u):
+            t = sb.tile([P, S, 2], BF16, name="b_pairs%d%d" % (z, u))
+            pairs[(z, u)] = t
+            for n in range(len(chunks[(z, u)])):
+                src, c0, w = raw[(z, u, n)]
+                view = src[:].rearrange("p e s -> p s e")
+                if w < 256:
+                    nc.vector.tensor_copy(t[:, c0 : c0 + w, :], view)
+                else:
+                    nc.scalar.activation(t[:, c0 : c0 + w, :], view, ACT.Copy)
+
+        def gather_b(z, u, dst, cols):
+            window = pairs[(z, u)][:].rearrange("p s e -> p (s e)").bitcast(F32)
+            nc.vector.tensor_copy(dst, window.indirect(list_b[:, cols.start // LIST_ROWS : cols.stop // LIST_ROWS]))
+
+        a_codes = [sb.tile([P, J], U32, name="a_codes%d" % z, align_bytes=64) for z in range(PASSES)]
+        a_planes = sb.tile([P, J], U8, name="a_planes", align_bytes=64)
+
+        def gather_a(z, cols):
+            nc.vector.tensor_copy(
+                a_codes[z][:, cols],
+                a_words[z][:].bitcast(U32).indirect(list_a[:, cols.start // LIST_ROWS : cols.stop // LIST_ROWS]),
+            )
+
+        gather_a(0, slice(0, J))
+        nc.vector.tensor_copy(a_planes[:], a_scales[:].indirect(list_a[:]))
+
+        cw_bank = ps.tile([P, PACK, P], F32, name="cw_bank")
+        for b in range(PACK):
+            nc.tensor.transpose(cw_bank[:, b, :], cw_rows[:, b : b + 1].to_broadcast([P, P]), identity[:])
+
+        acc = [ps.tile([P, I], F32, name="acc%d" % j) for j in range(J_TILES)]
+
+        def multiply(z, j, cols, codes, planes, start, stop):
+            rows = slice(j * P, (j + 1) * P)
+            nc.tensor.matmul_mx(
+                acc[j][:, cols],
+                lhsT=a_codes[z][:, rows].bitcast(FP8X4),
+                lhsT_scale=a_planes[4 * z : P, rows],
+                rhs=codes[:].bitcast(FP8X4),
+                rhs_scale=planes[:],
+                start=start,
+                stop=stop,
+            )
+
+        def quantize(name, width, woven):
+            codes = sb.tile([P, width], U32, name="b_codes" + name, align_bytes=64)
+            planes = sb.tile([P, width], U8, name="b_planes" + name, align_bytes=64)
+            nc.vector.quantize_mx(codes[:].bitcast(FP8X4), planes[:], woven[:])
+            return codes, planes
+
+        picked0 = sb.tile([P, 2, I], F32, name="picked0")
+        for u in range(2):
+            cast_b(0, u)
+            gather_b(0, u, picked0[:, u, :], slice(0, I))
+        woven0 = sb.tile([P, I * PACK], BF16, name="woven0", align_bytes=64)
+        nc.vector.tensor_copy(
+            woven0[:].bitcast(F32).rearrange("p (i u) -> p i u", u=2), picked0[:].rearrange("p u i -> p i u")
+        )
+        cast_b(1, 0)
+        codes0, planes0 = quantize("0", I, woven0)
+        for j in range(J_TILES):
+            multiply(0, j, slice(0, I), codes0, planes0, True, False)
+
+        halves = [slice(0, HALF), slice(HALF, I)]
+        picked1 = [sb.tile([P, 2, HALF], F32, name="picked1%d" % h) for h in range(2)]
+        for h in range(2):
+            gather_b(1, 0, picked1[h][:, 0, :], halves[h])
+        cast_b(1, 1)
+        woven1 = [sb.tile([P, HALF * PACK], BF16, name="woven1%d" % h, align_bytes=64) for h in range(2)]
+        for h in range(2):
+            gather_b(1, 1, picked1[h][:, 1, :], halves[h])
+            nc.scalar.copy(
+                woven1[h][:].bitcast(F32).rearrange("p (i u) -> p i u", u=2), picked1[h][:].rearrange("p u i -> p i u")
+            )
+        gather_a(1, slice(0, P))
+        quantized = [quantize("1%d" % h, HALF, woven1[h]) for h in range(2)]
+        for j in range(1, J_TILES):
+            gather_a(1, slice(j * P, (j + 1) * P))
+
+        cw_view = cw_bank[:].rearrange("p b q -> p q b")
+        for j in range(J_TILES):
+            for h in range(2):
+                multiply(1, j, halves[h], quantized[h][0], quantized[h][1], False, h == 1)
+            relu = sb.tile([P, I], F32, name="relu%d" % j)
+            total = sb.tile([P, 1], F32, name="total%d" % j)
+            nc.scalar.activation(relu[:], acc[j][:], ACT.Relu, accum_out=total[:])
+            denom = sb.tile([P, 1], F32, name="denom%d" % j)
+            nc.vector.tensor_scalar(denom[:], total[:], 1.0, None, ALU.add)
+            inv = sb.tile([P, 1], F32, name="inv%d" % j)
+            nc.vector.reciprocal(inv[:], denom[:])
+            pieces = halves if j == J_TILES - 1 else [slice(0, I)]
+            for n, cols in enumerate(pieces):
+                w = cols.stop - cols.start
+                res = sb.tile([P, w], F32, name="res%d%d" % (j, n))
+                nc.vector.scalar_tensor_tensor(
+                    res[:].rearrange("p (q b) -> p q b", b=PACK),
+                    relu[:, cols].rearrange("p (q b) -> p q b", b=PACK),
+                    inv[:],
+                    cw_view[:, cols.start // PACK : cols.stop // PACK, :],
+                    ALU.mult,
+                    ALU.mult,
+                )
+                nc.sync.dma_start(out[j * P : (j + 1) * P, cols], res[:])

@@ -32,8 +32,6 @@ def tile_list_affinity_of_two_lists_kernel(tc, xa_words, xa_scales, xb, cw1, off
 
         list_a = sb.tile([P, J // LIST_ROWS], U16, name="list_a")
         list_b = sb.tile([P, I // LIST_ROWS], U16, name="list_b")
-        nc.sync.dma_start(list_a[:], offs)
-        nc.sync.dma_start(list_b[:], offs2)
 
         a_words = [sb.tile([P, T], I32, name="a_words%d" % z) for z in range(PASSES)]
 
@@ -41,19 +39,22 @@ def tile_list_affinity_of_two_lists_kernel(tc, xa_words, xa_scales, xb, cw1, off
             nc.sync.dma_start(a_words[z][:], xa_words[z].rearrange("p t r -> p (t r)").bitcast(I32))
 
         a_scales = sb.tile([P, T], U8, name="a_scales")
-        nc.vector.memset(a_scales[:].bitcast(I32), 0)
+        nc.gpsimd.memset(a_scales[:].bitcast(I32), 0)
+        nc.sync.dma_start(list_a[:], offs)
+        load_a_words(0)
         for q in range(4):
-            nc.scalar.dma_start(
+            nc.sync.dma_start(
                 a_scales[32 * q : 32 * q + 4 * PASSES, :].bitcast(I32),
                 xa_scales[:, 4 * q : 4 * q + 4, :].bitcast(I32),
             )
         cw_rows = sb.tile([P, PACK], F32, name="cw_rows")
-        nc.scalar.dma_start(cw_rows[:], cw1.rearrange("o (p b) -> (o p) b", b=PACK))
+        nc.sync.dma_start(list_b[:], offs2)
         identity = sb.tile([P, P], F32, name="identity")
         make_identity(nc, identity[:])
 
         xb_rows = xb.rearrange("(z p u e) s -> z u p e s", z=PASSES, u=2, e=2)
-        chunks = {(0, 0): [512, 512], (0, 1): [512, 512], (1, 0): [512, 512], (1, 1): [512, 384, 128]}
+        chunks = {(0, 0): [512, 512], (0, 1): [512, 512], (1, 0): [384, 384, 256], (1, 1): [384, 384, 256]}
+        on_vector = {(0, 0): 320, (0, 1): 320, (1, 0): 0, (1, 1): 256}
         raw = {}
 
         def load_b(z, u):
@@ -64,39 +65,46 @@ def tile_list_affinity_of_two_lists_kernel(tc, xa_words, xa_scales, xb, cw1, off
                 raw[(z, u, n)] = (t, c0, w)
                 c0 += w
 
-        load_a_words(0)
-        for z in range(PASSES):
-            for u in range(2):
-                load_b(z, u)
+        load_b(0, 0)
+        nc.sync.dma_start(cw_rows[:], cw1.rearrange("o (p b) -> (o p) b", b=PACK))
+        load_b(0, 1)
+        load_b(1, 0)
+        load_b(1, 1)
         load_a_words(1)
 
         pairs = {}
 
         def cast_b(z, u):
-            t = sb.tile([P, S, 2], BF16, name="b_pairs%d%d" % (z, u))
+            t = sb.tile([P, S, 2], BF16, name="b_pairs%d%d" % (z, u), tag="b_pairs%d%d" % (z, u), align_bytes=64)
             pairs[(z, u)] = t
             for n in range(len(chunks[(z, u)])):
                 src, c0, w = raw[(z, u, n)]
                 view = src[:].rearrange("p e s -> p s e")
-                if w < 256:
-                    nc.vector.tensor_copy(t[:, c0 : c0 + w, :], view)
-                else:
-                    nc.scalar.activation(t[:, c0 : c0 + w, :], view, ACT.Copy)
+                ws = min(w, S - on_vector[(z, u)] - c0)
+                if ws > 0:
+                    nc.scalar.activation(t[:, c0 : c0 + ws, :], view[:, 0:ws, :], ACT.Copy)
+                if ws < w:
+                    nc.vector.tensor_copy(t[:, c0 + ws : c0 + w, :], view[:, ws:w, :])
 
         def gather_b(z, u, dst, cols):
             window = pairs[(z, u)][:].rearrange("p s e -> p (s e)").bitcast(F32)
             nc.vector.tensor_copy(dst, window.indirect(list_b[:, cols.start // LIST_ROWS : cols.stop // LIST_ROWS]))
 
-        a_codes = [sb.tile([P, J], U32, name="a_codes%d" % z, align_bytes=64) for z in range(PASSES)]
+        a_codes = {}
         a_planes = sb.tile([P, J], U8, name="a_planes", align_bytes=64)
 
-        def gather_a(z, cols):
-            nc.vector.tensor_copy(
-                a_codes[z][:, cols],
-                a_words[z][:].bitcast(U32).indirect(list_a[:, cols.start // LIST_ROWS : cols.stop // LIST_ROWS]),
-            )
+        def gather_a(z, cuts, tag):
+            first, last = cuts[0].start, cuts[-1].stop
+            t = sb.tile([P, last - first], U32, name="a_codes%d_%d" % (z, first), tag=tag, align_bytes=64)
+            for c in range(first, last, P):
+                a_codes[(z, c // P)] = t[:, c - first : c - first + P]
+            for cols in cuts:
+                nc.vector.tensor_copy(
+                    t[:, cols.start - first : cols.stop - first],
+                    a_words[z][:].bitcast(U32).indirect(list_a[:, cols.start // LIST_ROWS : cols.stop // LIST_ROWS]),
+                )
 
-        gather_a(0, slice(0, J))
+        gather_a(0, [slice(0, J)], "a_codes0")
         nc.vector.tensor_copy(a_planes[:], a_scales[:].indirect(list_a[:]))
 
         cw_bank = ps.tile([P, PACK, P], F32, name="cw_bank")
@@ -105,74 +113,85 @@ def tile_list_affinity_of_two_lists_kernel(tc, xa_words, xa_scales, xb, cw1, off
 
         acc = [ps.tile([P, I], F32, name="acc%d" % j) for j in range(J_TILES)]
 
-        def multiply(z, j, cols, codes, planes, start, stop):
+        b_codes = [sb.tile([P, I], U32, name="b_codes%d" % z, align_bytes=64) for z in range(PASSES)]
+        b_planes = [sb.tile([P, I], U8, name="b_planes%d" % z, align_bytes=64) for z in range(PASSES)]
+
+        def multiply(z, j, cols, start, stop):
             rows = slice(j * P, (j + 1) * P)
             nc.tensor.matmul_mx(
                 acc[j][:, cols],
-                lhsT=a_codes[z][:, rows].bitcast(FP8X4),
+                lhsT=a_codes[(z, j)].bitcast(FP8X4),
                 lhsT_scale=a_planes[4 * z : P, rows],
-                rhs=codes[:].bitcast(FP8X4),
-                rhs_scale=planes[:],
+                rhs=b_codes[z][:, cols].bitcast(FP8X4),
+                rhs_scale=b_planes[z][:, cols],
                 start=start,
                 stop=stop,
             )
 
-        def quantize(name, width, woven):
-            codes = sb.tile([P, width], U32, name="b_codes" + name, align_bytes=64)
-            planes = sb.tile([P, width], U8, name="b_planes" + name, align_bytes=64)
-            nc.vector.quantize_mx(codes[:].bitcast(FP8X4), planes[:], woven[:])
-            return codes, planes
+        halves = [slice(0, HALF), slice(HALF, I)]
+        pieces = [halves, [slice(0, 256), slice(256, 384), slice(384, 512)]]
+        picked, woven = {}, {}
+        for z in range(PASSES):
+            for n, cols in enumerate(pieces[z]):
+                w = cols.stop - cols.start
+                picked[(z, n)] = sb.tile([P, 2, w], F32, name="picked%d%d" % (z, n))
+                woven[(z, n)] = sb.tile([P, w * PACK], BF16, name="woven%d%d" % (z, n), tag="woven%d%d" % (z, n), align_bytes=64)
 
-        picked0 = sb.tile([P, 2, I], F32, name="picked0")
+        def weave(z, n, copy):
+            copy(woven[(z, n)][:].bitcast(F32).rearrange("p (i u) -> p i u", u=2), picked[(z, n)][:].rearrange("p u i -> p i u"))
+
+        def quantize(z, n):
+            cols = pieces[z][n]
+            nc.vector.quantize_mx(b_codes[z][:, cols].bitcast(FP8X4), b_planes[z][:, cols], woven[(z, n)][:])
+
         for u in range(2):
             cast_b(0, u)
-            gather_b(0, u, picked0[:, u, :], slice(0, I))
-        woven0 = sb.tile([P, I * PACK], BF16, name="woven0", align_bytes=64)
-        nc.vector.tensor_copy(
-            woven0[:].bitcast(F32).rearrange("p (i u) -> p i u", u=2), picked0[:].rearrange("p u i -> p i u")
-        )
-        cast_b(1, 0)
-        codes0, planes0 = quantize("0", I, woven0)
+            for n, cols in enumerate(pieces[0]):
+                gather_b(0, u, picked[(0, n)][:, u, :], cols)
+        for n in range(2):
+            weave(0, n, nc.vector.tensor_copy)
+        for n in range(2):
+            quantize(0, n)
         for j in range(J_TILES):
-            multiply(0, j, slice(0, I), codes0, planes0, True, False)
+            multiply(0, j, slice(0, I), True, False)
 
-        halves = [slice(0, HALF), slice(HALF, I)]
-        picked1 = [sb.tile([P, 2, HALF], F32, name="picked1%d" % h) for h in range(2)]
-        for h in range(2):
-            gather_b(1, 0, picked1[h][:, 0, :], halves[h])
+        cast_b(1, 0)
+        for n, cols in enumerate(pieces[1]):
+            gather_b(1, 0, picked[(1, n)][:, 0, :], cols)
         cast_b(1, 1)
-        woven1 = [sb.tile([P, HALF * PACK], BF16, name="woven1%d" % h, align_bytes=64) for h in range(2)]
-        for h in range(2):
-            gather_b(1, 1, picked1[h][:, 1, :], halves[h])
-            nc.scalar.copy(
-                woven1[h][:].bitcast(F32).rearrange("p (i u) -> p i u", u=2), picked1[h][:].rearrange("p u i -> p i u")
-            )
-        gather_a(1, slice(0, P))
-        quantized = [quantize("1%d" % h, HALF, woven1[h]) for h in range(2)]
-        for j in range(1, J_TILES):
-            gather_a(1, slice(j * P, (j + 1) * P))
+        for n, cols in enumerate(pieces[1]):
+            gather_b(1, 1, picked[(1, n)][:, 1, :], cols)
+            weave(1, n, nc.scalar.copy)
+        gather_a(1, [slice(0, P)], "b_pairs11")
+        for n in range(len(pieces[1])):
+            quantize(1, n)
+        gather_a(1, [slice(P, 2 * P), slice(2 * P, J)], "woven12")
 
         cw_view = cw_bank[:].rearrange("p b q -> p q b")
+        relu, inv = [], []
         for j in range(J_TILES):
-            for h in range(2):
-                multiply(1, j, halves[h], quantized[h][0], quantized[h][1], False, h == 1)
-            relu = sb.tile([P, I], F32, name="relu%d" % j)
+            cuts = pieces[1] if j == 0 else [slice(0, I)]
+            for cols in cuts:
+                multiply(1, j, cols, False, cols.stop == I)
+            relu.append(sb.tile([P, I], F32, name="relu%d" % j))
             total = sb.tile([P, 1], F32, name="total%d" % j)
-            nc.scalar.activation(relu[:], acc[j][:], ACT.Relu, accum_out=total[:])
+            nc.scalar.activation(relu[j][:], acc[j][:], ACT.Relu, accum_out=total[:])
             denom = sb.tile([P, 1], F32, name="denom%d" % j)
             nc.vector.tensor_scalar(denom[:], total[:], 1.0, None, ALU.add)
-            inv = sb.tile([P, 1], F32, name="inv%d" % j)
-            nc.vector.reciprocal(inv[:], denom[:])
-            pieces = halves if j == J_TILES - 1 else [slice(0, I)]
-            for n, cols in enumerate(pieces):
-                w = cols.stop - cols.start
-                res = sb.tile([P, w], F32, name="res%d%d" % (j, n))
+            inv.append(sb.tile([P, 1], F32, name="inv%d" % j))
+            nc.vector.reciprocal(inv[j][:], denom[:])
+        for j in range(J_TILES):
+            res = sb.tile([P, I], F32, name="res%d" % j)
+            for cols in halves:
                 nc.vector.scalar_tensor_tensor(
-                    res[:].rearrange("p (q b) -> p q b", b=PACK),
-                    relu[:, cols].rearrange("p (q b) -> p q b", b=PACK),
-                    inv[:],
+                    res[:, cols].rearrange("p (q b) -> p q b", b=PACK),
+                    relu[j][:, cols].rearrange("p (q b) -> p q b", b=PACK),
+                    inv[j][:],
                     cw_view[:, cols.start // PACK : cols.stop // PACK, :],
                     ALU.mult,
                     ALU.mult,
                 )
-                nc.sync.dma_start(out[j * P : (j + 1) * P, cols], res[:])
+                if j == J_TILES - 1:
+                    nc.sync.dma_start(out[j * P : (j + 1) * P, cols], res[:, cols])
+            if j < J_TILES - 1:
+                nc.sync.dma_start(out[j * P : (j + 1) * P, :], res[:])

@@ -40,21 +40,19 @@ def tile_list_affinity_of_two_lists_kernel(tc, xa_words, xa_scales, xb, cw1, off
 
         a_scales = sb.tile([P, T], U8, name="a_scales")
         nc.gpsimd.memset(a_scales[:].bitcast(I32), 0)
-        nc.sync.dma_start(list_a[:], offs)
         load_a_words(0)
+        nc.sync.dma_start(list_a[:], offs)
         for q in range(4):
             nc.sync.dma_start(
                 a_scales[32 * q : 32 * q + 4 * PASSES, :].bitcast(I32),
                 xa_scales[:, 4 * q : 4 * q + 4, :].bitcast(I32),
             )
-        cw_rows = sb.tile([P, PACK], F32, name="cw_rows")
-        nc.sync.dma_start(list_b[:], offs2)
         identity = sb.tile([P, P], F32, name="identity")
         make_identity(nc, identity[:])
 
         xb_rows = xb.rearrange("(z p u e) s -> z u p e s", z=PASSES, u=2, e=2)
-        chunks = {(0, 0): [512, 512], (0, 1): [512, 512], (1, 0): [384, 384, 256], (1, 1): [384, 384, 256]}
-        on_vector = {(0, 0): 320, (0, 1): 320, (1, 0): 0, (1, 1): 256}
+        chunks = {(0, 0): [1024], (0, 1): [1024], (1, 0): [1024], (1, 1): [512, 512]}
+        on_vector = {(0, 0): 576, (0, 1): 640, (1, 0): 576, (1, 1): 320}
         raw = {}
 
         def load_b(z, u):
@@ -66,11 +64,17 @@ def tile_list_affinity_of_two_lists_kernel(tc, xa_words, xa_scales, xb, cw1, off
                 c0 += w
 
         load_b(0, 0)
-        nc.sync.dma_start(cw_rows[:], cw1.rearrange("o (p b) -> (o p) b", b=PACK))
+        nc.sync.dma_start(list_b[:], offs2)
         load_b(0, 1)
+        cw_rows = sb.tile([P, PACK], F32, name="cw_rows")
+        nc.sync.dma_start(cw_rows[:], cw1.rearrange("o (p b) -> (o p) b", b=PACK))
         load_b(1, 0)
         load_b(1, 1)
         load_a_words(1)
+
+        cw_all = ps.tile([P, I], F32, name="cw_all")
+        for b in range(PACK):
+            nc.tensor.transpose(cw_all[:, b:I:PACK], cw_rows[:, b : b + 1].to_broadcast([P, P]), identity[:])
 
         pairs = {}
 
@@ -107,10 +111,6 @@ def tile_list_affinity_of_two_lists_kernel(tc, xa_words, xa_scales, xb, cw1, off
         gather_a(0, [slice(0, J)], "a_codes0")
         nc.vector.tensor_copy(a_planes[:], a_scales[:].indirect(list_a[:]))
 
-        cw_bank = ps.tile([P, PACK, P], F32, name="cw_bank")
-        for b in range(PACK):
-            nc.tensor.transpose(cw_bank[:, b, :], cw_rows[:, b : b + 1].to_broadcast([P, P]), identity[:])
-
         acc = [ps.tile([P, I], F32, name="acc%d" % j) for j in range(J_TILES)]
 
         b_codes = [sb.tile([P, I], U32, name="b_codes%d" % z, align_bytes=64) for z in range(PASSES)]
@@ -130,44 +130,46 @@ def tile_list_affinity_of_two_lists_kernel(tc, xa_words, xa_scales, xb, cw1, off
 
         halves = [slice(0, HALF), slice(HALF, I)]
         pieces = [halves, [slice(0, 256), slice(256, 384), slice(384, 512)]]
-        picked, woven = {}, {}
+        picked = [sb.tile([P, 2, I], F32, name="picked%d" % z) for z in range(PASSES)]
+        woven = {}
         for z in range(PASSES):
             for n, cols in enumerate(pieces[z]):
                 w = cols.stop - cols.start
-                picked[(z, n)] = sb.tile([P, 2, w], F32, name="picked%d%d" % (z, n))
                 woven[(z, n)] = sb.tile([P, w * PACK], BF16, name="woven%d%d" % (z, n), tag="woven%d%d" % (z, n), align_bytes=64)
 
         def weave(z, n, copy):
-            copy(woven[(z, n)][:].bitcast(F32).rearrange("p (i u) -> p i u", u=2), picked[(z, n)][:].rearrange("p u i -> p i u"))
+            copy(
+                woven[(z, n)][:].bitcast(F32).rearrange("p (i u) -> p i u", u=2),
+                picked[z][:, :, pieces[z][n]].rearrange("p u i -> p i u"),
+            )
 
         def quantize(z, n):
             cols = pieces[z][n]
             nc.vector.quantize_mx(b_codes[z][:, cols].bitcast(FP8X4), b_planes[z][:, cols], woven[(z, n)][:])
 
-        for u in range(2):
-            cast_b(0, u)
-            for n, cols in enumerate(pieces[0]):
-                gather_b(0, u, picked[(0, n)][:, u, :], cols)
+        cast_b(0, 0)
+        gather_b(0, 0, picked[0][:, 0, :], slice(0, I))
+        cast_b(0, 1)
+        for cols in pieces[0]:
+            gather_b(0, 1, picked[0][:, 1, cols], cols)
         for n in range(2):
-            weave(0, n, nc.vector.tensor_copy)
+            weave(0, n, nc.scalar.copy)
         for n in range(2):
             quantize(0, n)
         for j in range(J_TILES):
             multiply(0, j, slice(0, I), True, False)
 
         cast_b(1, 0)
-        for n, cols in enumerate(pieces[1]):
-            gather_b(1, 0, picked[(1, n)][:, 0, :], cols)
+        gather_b(1, 0, picked[1][:, 0, :], slice(0, I))
         cast_b(1, 1)
         for n, cols in enumerate(pieces[1]):
-            gather_b(1, 1, picked[(1, n)][:, 1, :], cols)
+            gather_b(1, 1, picked[1][:, 1, cols], cols)
             weave(1, n, nc.scalar.copy)
-        gather_a(1, [slice(0, P)], "b_pairs11")
         for n in range(len(pieces[1])):
             quantize(1, n)
-        gather_a(1, [slice(P, 2 * P), slice(2 * P, J)], "woven12")
+        gather_a(1, [slice(0, P)], "woven10")
+        gather_a(1, [slice(P, 2 * P), slice(2 * P, J)], "woven11")
 
-        cw_view = cw_bank[:].rearrange("p b q -> p q b")
         relu, inv = [], []
         for j in range(J_TILES):
             cuts = pieces[1] if j == 0 else [slice(0, I)]
@@ -184,12 +186,7 @@ def tile_list_affinity_of_two_lists_kernel(tc, xa_words, xa_scales, xb, cw1, off
             res = sb.tile([P, I], F32, name="res%d" % j)
             for cols in halves:
                 nc.vector.scalar_tensor_tensor(
-                    res[:, cols].rearrange("p (q b) -> p q b", b=PACK),
-                    relu[j][:, cols].rearrange("p (q b) -> p q b", b=PACK),
-                    inv[j][:],
-                    cw_view[:, cols.start // PACK : cols.stop // PACK, :],
-                    ALU.mult,
-                    ALU.mult,
+                    res[:, cols], relu[j][:, cols], inv[j][:], cw_all[:, cols], ALU.mult, ALU.mult
                 )
                 if j == J_TILES - 1:
                     nc.sync.dma_start(out[j * P : (j + 1) * P, cols], res[:, cols])

@@ -51,8 +51,8 @@ def tile_list_affinity_of_two_lists_kernel(tc, xa_words, xa_scales, xb, cw1, off
         make_identity(nc, identity[:])
 
         xb_rows = xb.rearrange("(z p u e) s -> z u p e s", z=PASSES, u=2, e=2)
-        chunks = {(0, 0): [1024], (0, 1): [1024], (1, 0): [1024], (1, 1): [512, 512]}
-        on_vector = {(0, 0): 576, (0, 1): 640, (1, 0): 576, (1, 1): 320}
+        chunks = {(0, 0): [1024], (0, 1): [512, 512], (1, 0): [512, 512], (1, 1): [512, 512]}
+        on_vector = {(0, 0): 640, (0, 1): 320, (1, 0): 0, (1, 1): 320}
         raw = {}
 
         def load_b(z, u):
@@ -111,24 +111,28 @@ def tile_list_affinity_of_two_lists_kernel(tc, xa_words, xa_scales, xb, cw1, off
         gather_a(0, [slice(0, J)], "a_codes0")
         nc.vector.tensor_copy(a_planes[:], a_scales[:].indirect(list_a[:]))
 
-        acc = [ps.tile([P, I], F32, name="acc%d" % j) for j in range(J_TILES)]
+        halves = [slice(0, HALF), slice(HALF, I)]
+        banks = [halves] + [[slice(0, I)]] * (J_TILES - 1)
+        acc = {}
+        for j in range(J_TILES):
+            for span in banks[j]:
+                acc[(j, span.start)] = ps.tile([P, span.stop - span.start], F32, name="acc%d_%d" % (j, span.start))
 
         b_codes = [sb.tile([P, I], U32, name="b_codes%d" % z, align_bytes=64) for z in range(PASSES)]
         b_planes = [sb.tile([P, I], U8, name="b_planes%d" % z, align_bytes=64) for z in range(PASSES)]
 
-        def multiply(z, j, cols, start, stop):
+        def multiply(z, j, span, cols):
             rows = slice(j * P, (j + 1) * P)
             nc.tensor.matmul_mx(
-                acc[j][:, cols],
+                acc[(j, span.start)][:, cols.start - span.start : cols.stop - span.start],
                 lhsT=a_codes[(z, j)].bitcast(FP8X4),
                 lhsT_scale=a_planes[4 * z : P, rows],
                 rhs=b_codes[z][:, cols].bitcast(FP8X4),
                 rhs_scale=b_planes[z][:, cols],
-                start=start,
-                stop=stop,
+                start=(z == 0),
+                stop=(z == PASSES - 1 and cols.stop == span.stop),
             )
 
-        halves = [slice(0, HALF), slice(HALF, I)]
         pieces = [halves, [slice(0, 256), slice(256, 384), slice(384, 512)]]
         picked = [sb.tile([P, 2, I], F32, name="picked%d" % z) for z in range(PASSES)]
         woven = {}
@@ -153,11 +157,12 @@ def tile_list_affinity_of_two_lists_kernel(tc, xa_words, xa_scales, xb, cw1, off
         for cols in pieces[0]:
             gather_b(0, 1, picked[0][:, 1, cols], cols)
         for n in range(2):
-            weave(0, n, nc.scalar.copy)
+            weave(0, n, nc.vector.tensor_copy)
         for n in range(2):
             quantize(0, n)
         for j in range(J_TILES):
-            multiply(0, j, slice(0, I), True, False)
+            for span in banks[j]:
+                multiply(0, j, span, span)
 
         cast_b(1, 0)
         gather_b(1, 0, picked[1][:, 0, :], slice(0, I))
@@ -168,18 +173,23 @@ def tile_list_affinity_of_two_lists_kernel(tc, xa_words, xa_scales, xb, cw1, off
         for n in range(len(pieces[1])):
             quantize(1, n)
         gather_a(1, [slice(0, P)], "woven10")
-        gather_a(1, [slice(P, 2 * P), slice(2 * P, J)], "woven11")
+        gather_a(1, [slice(P, 2 * P), slice(2 * P, J)], "woven12")
 
         relu, inv = [], []
         for j in range(J_TILES):
-            cuts = pieces[1] if j == 0 else [slice(0, I)]
-            for cols in cuts:
-                multiply(1, j, cols, False, cols.stop == I)
             relu.append(sb.tile([P, I], F32, name="relu%d" % j))
-            total = sb.tile([P, 1], F32, name="total%d" % j)
-            nc.scalar.activation(relu[j][:], acc[j][:], ACT.Relu, accum_out=total[:])
+            totals = []
+            for span in banks[j]:
+                cuts = [c for c in pieces[1] if span.start <= c.start < span.stop] if j == 0 else [span]
+                for cols in cuts:
+                    multiply(1, j, span, cols)
+                totals.append(sb.tile([P, 1], F32, name="total%d_%d" % (j, span.start)))
+                nc.scalar.activation(relu[j][:, span], acc[(j, span.start)][:], ACT.Relu, accum_out=totals[-1][:])
             denom = sb.tile([P, 1], F32, name="denom%d" % j)
-            nc.vector.tensor_scalar(denom[:], total[:], 1.0, None, ALU.add)
+            if j == 0:
+                nc.vector.tensor_scalar(denom[:], totals[0][:], totals[1][:], 1.0, ALU.add, ALU.add)
+            else:
+                nc.vector.tensor_scalar(denom[:], totals[0][:], 1.0, None, ALU.add)
             inv.append(sb.tile([P, 1], F32, name="inv%d" % j))
             nc.vector.reciprocal(inv[j][:], denom[:])
         for j in range(J_TILES):

from contextlib import ExitStack

import concourse.mybir as mybir
from concourse.masks import make_identity

K, T, S, J, I = 1024, 1024, 1024, 512, 512
FLOPS = 2 * K * J * I

F32 = mybir.dt.float32
BF16 = mybir.dt.bfloat16
I32 = mybir.dt.int32
U32 = mybir.dt.uint32
U16 = mybir.dt.uint16
U8 = mybir.dt.uint8
FP8X4 = mybir.dt.float8_e4m3fn_x4
ALU = mybir.AluOpType
ACT = mybir.ActivationFunctionType

P = 128
PACK = 4
PASSES = 2
HALF = I // 2
J_TILES = J // P
LIST_ROWS = 16


def tile_list_affinity_of_two_lists_kernel(tc, xa_words, xa_scales, xb, cw1, offs, offs2, out):
    nc = tc.nc
    with ExitStack() as ctx:
        sb = ctx.enter_context(tc.tile_pool(name="sb", bufs=1))
        ps = ctx.enter_context(tc.psum_pool(name="ps", bufs=1))

        list_a = sb.tile([P, J // LIST_ROWS], U16, name="list_a")
        list_b = sb.tile([P, I // LIST_ROWS], U16, name="list_b")

        a_words = [sb.tile([P, T], I32, name="a_words%d" % z) for z in range(PASSES)]

        def load_a_words(z):
            nc.sync.dma_start(a_words[z][:], xa_words[z].rearrange("p t r -> p (t r)").bitcast(I32))

        a_scales = sb.tile([P, T], U8, name="a_scales")
        nc.gpsimd.memset(a_scales[:].bitcast(I32), 0)
        load_a_words(0)
        nc.sync.dma_start(list_a[:], offs)
        for q in range(4):
            nc.sync.dma_start(
                a_scales[32 * q : 32 * q + 4 * PASSES, :].bitcast(I32),
                xa_scales[:, 4 * q : 4 * q + 4, :].bitcast(I32),
            )
        identity = sb.tile([P, P], F32, name="identity")
        make_identity(nc, identity[:])

        xb_rows = xb.rearrange("(z p u e) s -> z u p e s", z=PASSES, u=2, e=2)
        chunks = {(0, 0): [1024], (0, 1): [512, 512], (1, 0): [512, 512], (1, 1): [512, 512]}
        on_vector = {(0, 0): 640, (0, 1): 320, (1, 0): 0, (1, 1): 320}
        raw = {}

        def load_b(z, u):
            c0 = 0
            for n, w in enumerate(chunks[(z, u)]):
                t = sb.tile([P, 2, w], F32, name="b_raw%d%d%d" % (z, u, n))
                nc.sync.dma_start(t[:], xb_rows[z, u, :, :, c0 : c0 + w])
                raw[(z, u, n)] = (t, c0, w)
                c0 += w

        load_b(0, 0)
        nc.sync.dma_start(list_b[:], offs2)
        load_b(0, 1)
        cw_rows = sb.tile([P, PACK], F32, name="cw_rows")
        nc.sync.dma_start(cw_rows[:], cw1.rearrange("o (p b) -> (o p) b", b=PACK))
        load_b(1, 0)
        load_b(1, 1)
        load_a_words(1)

        cw_all = ps.tile([P, I], F32, name="cw_all")
        for b in range(PACK):
            nc.tensor.transpose(cw_all[:, b:I:PACK], cw_rows[:, b : b + 1].to_broadcast([P, P]), identity[:])

        pairs = {}

        def cast_b(z, u):
            t = sb.tile([P, S, 2], BF16, name="b_pairs%d%d" % (z, u), tag="b_pairs%d%d" % (z, u), align_bytes=64)
            pairs[(z, u)] = t
            for n in range(len(chunks[(z, u)])):
                src, c0, w = raw[(z, u, n)]
                view = src[:].rearrange("p e s -> p s e")
                ws = min(w, S - on_vector[(z, u)] - c0)
                if ws > 0:
                    nc.scalar.activation(t[:, c0 : c0 + ws, :], view[:, 0:ws, :], ACT.Copy)
                if ws < w:
                    nc.vector.tensor_copy(t[:, c0 + ws : c0 + w, :], view[:, ws:w, :])

        def gather_b(z, u, dst, cols):
            window = pairs[(z, u)][:].rearrange("p s e -> p (s e)").bitcast(F32)
            nc.vector.tensor_copy(dst, window.indirect(list_b[:, cols.start // LIST_ROWS : cols.stop // LIST_ROWS]))

        a_codes = {}
        a_planes = sb.tile([P, J], U8, name="a_planes", align_bytes=64)

        def gather_a(z, cuts, tag):
            first, last = cuts[0].start, cuts[-1].stop
            t = sb.tile([P, last - first], U32, name="a_codes%d_%d" % (z, first), tag=tag, align_bytes=64)
            for c in range(first, last, P):
                a_codes[(z, c // P)] = t[:, c - first : c - first + P]
            for cols in cuts:
                nc.vector.tensor_copy(
                    t[:, cols.start - first : cols.stop - first],
                    a_words[z][:].bitcast(U32).indirect(list_a[:, cols.start // LIST_ROWS : cols.stop // LIST_ROWS]),
                )

        gather_a(0, [slice(0, J)], "a_codes0")
        nc.vector.tensor_copy(a_planes[:], a_scales[:].indirect(list_a[:]))

        halves = [slice(0, HALF), slice(HALF, I)]
        banks = [halves] + [[slice(0, I)]] * (J_TILES - 1)
        acc = {}
        for j in range(J_TILES):
            for span in banks[j]:
                acc[(j, span.start)] = ps.tile([P, span.stop - span.start], F32, name="acc%d_%d" % (j, span.start))

        b_codes = [sb.tile([P, I], U32, name="b_codes%d" % z, align_bytes=64) for z in range(PASSES)]
        b_planes = [sb.tile([P, I], U8, name="b_planes%d" % z, align_bytes=64) for z in range(PASSES)]

        def multiply(z, j, span, cols):
            rows = slice(j * P, (j + 1) * P)
            nc.tensor.matmul_mx(
                acc[(j, span.start)][:, cols.start - span.start : cols.stop - span.start],
                lhsT=a_codes[(z, j)].bitcast(FP8X4),
                lhsT_scale=a_planes[4 * z : P, rows],
                rhs=b_codes[z][:, cols].bitcast(FP8X4),
                rhs_scale=b_planes[z][:, cols],
                start=(z == 0),
                stop=(z == PASSES - 1 and cols.stop == span.stop),
            )

        pieces = [halves, [slice(0, 256), slice(256, 384), slice(384, 512)]]
        picked = [sb.tile([P, 2, I], F32, name="picked%d" % z) for z in range(PASSES)]
        woven = {}
        for z in range(PASSES):
            for n, cols in enumerate(pieces[z]):
                w = cols.stop - cols.start
                woven[(z, n)] = sb.tile([P, w * PACK], BF16, name="woven%d%d" % (z, n), tag="woven%d%d" % (z, n), align_bytes=64)

        def weave(z, n, copy):
            copy(
                woven[(z, n)][:].bitcast(F32).rearrange("p (i u) -> p i u", u=2),
                picked[z][:, :, pieces[z][n]].rearrange("p u i -> p i u"),
            )

        def quantize(z, n):
            cols = pieces[z][n]
            nc.vector.quantize_mx(b_codes[z][:, cols].bitcast(FP8X4), b_planes[z][:, cols], woven[(z, n)][:])

        cast_b(0, 0)
        gather_b(0, 0, picked[0][:, 0, :], slice(0, I))
        cast_b(0, 1)
        for cols in pieces[0]:
            gather_b(0, 1, picked[0][:, 1, cols], cols)
        for n in range(2):
            weave(0, n, nc.vector.tensor_copy)
        for n in range(2):
            quantize(0, n)
        for j in range(J_TILES):
            for span in banks[j]:
                multiply(0, j, span, span)

        cast_b(1, 0)
        gather_b(1, 0, picked[1][:, 0, :], slice(0, I))
        cast_b(1, 1)
        for n, cols in enumerate(pieces[1]):
            gather_b(1, 1, picked[1][:, 1, cols], cols)
            weave(1, n, nc.scalar.copy)
        for n in range(len(pieces[1])):
            quantize(1, n)
        gather_a(1, [slice(0, P)], "woven10")
        gather_a(1, [slice(P, 2 * P), slice(2 * P, J)], "woven12")

        relu, inv = [], []
        for j in range(J_TILES):
            relu.append(sb.tile([P, I], F32, name="relu%d" % j))
            totals = []
            for span in banks[j]:
                cuts = [c for c in pieces[1] if span.start <= c.start < span.stop] if j == 0 else [span]
                for cols in cuts:
                    multiply(1, j, span, cols)
                totals.append(sb.tile([P, 1], F32, name="total%d_%d" % (j, span.start)))
                nc.scalar.activation(relu[j][:, span], acc[(j, span.start)][:], ACT.Relu, accum_out=totals[-1][:])
            denom = sb.tile([P, 1], F32, name="denom%d" % j)
            if j == 0:
                nc.vector.tensor_scalar(denom[:], totals[0][:], totals[1][:], 1.0, ALU.add, ALU.add)
            else:
                nc.vector.tensor_scalar(denom[:], totals[0][:], 1.0, None, ALU.add)
            inv.append(sb.tile([P, 1], F32, name="inv%d" % j))
            nc.vector.reciprocal(inv[j][:], denom[:])
        for j in range(J_TILES):
            res = sb.tile([P, I], F32, name="res%d" % j)
            for cols in halves:
                nc.vector.scalar_tensor_tensor(
                    res[:, cols], relu[j][:, cols], inv[j][:], cw_all[:, cols], ALU.mult, ALU.mult
                )
                if j == J_TILES - 1:
                    nc.sync.dma_start(out[j * P : (j + 1) * P, cols], res[:, cols])
            if j < J_TILES - 1:
                nc.sync.dma_start(out[j * P : (j + 1) * P, :], res[:])
